import numpy as np
import ml_dtypes


def mxq(x, axis, fmt="e4m3"):
    dtype, down = {"e4m3": (ml_dtypes.float8_e4m3fn, 7), "e5m2": (ml_dtypes.float8_e5m2, 14)}[fmt]
    v = np.moveaxis(np.asarray(x, np.float32).astype(ml_dtypes.bfloat16).astype(np.float64), axis, -1)
    blocks = v.reshape(v.shape[:-1] + (-1, 32))
    amax = np.abs(blocks).max(-1, keepdims=True)
    byte = np.maximum(np.where(amax > 0, np.frexp(amax)[1] - 1 + 127, 0) - down, 1)
    scale = np.exp2(byte - 127.0)
    codes = (blocks / scale).astype(np.float32).astype(dtype).astype(np.float64)
    return np.moveaxis((codes * scale).reshape(v.shape), -1, axis)


WIDE = False


def mx_kscale(k):
    if not WIDE:
        return np.ones(k)
    levels = np.array([10, -10, 5, -5, 0])
    if k % 512:
        return np.exp2(np.random.permutation(np.resize(levels, k // 32))).repeat(32)
    a = np.empty((k // 512, 16))
    for p in range(k // 512):
        a[p, :8] = np.random.permutation(np.resize(levels, 8))
        for g in range(8):
            far = levels[np.abs(levels - a[p, g]) >= 10]
            a[p, g + 8] = far[np.random.randint(len(far))]
    return np.exp2(a.ravel()).repeat(32)


def f64(x):
    return np.asarray(x).astype(np.float64)


def striped(idx):
    return np.tile(idx.reshape(-1, 16).T, (8, 1)).astype(np.uint16)


def unstriped(offs):
    return offs[:16].T.reshape(-1).astype(np.int64)


def pack_weight(w):
    k, n = w.shape
    w = f64(np.asarray(w, np.float32).astype(ml_dtypes.bfloat16)).reshape(k // 32, 32, n)
    amax = np.abs(w).max(1)
    byte = np.clip(np.where(amax > 0, np.frexp(amax)[1] - 1 + 127 - 7, 1), 1, 254)
    scaled = (w * np.exp2(127.0 - byte)[:, None, :]).reshape(k, n).astype(np.float32)
    words = np.ascontiguousarray(scaled.reshape(k // 512, 128, 4, n).transpose(0, 1, 3, 2)).astype(ml_dtypes.float8_e4m3fn).view(np.uint8)
    return words, np.ascontiguousarray(byte.astype(np.uint8).reshape(k // 512, 16, n))


def unpack_weight(words, scales):
    g, p, n, _ = words.shape
    vals = np.ascontiguousarray(words).view(ml_dtypes.float8_e4m3fn).astype(np.float64) * np.repeat(np.exp2(scales.astype(np.float64) - 127.0), 8, axis=1)[..., None]
    return vals.transpose(0, 1, 3, 2).reshape(g * 512, n)


def sigmoid(v):
    return 1.0 / (1.0 + np.exp(-np.maximum(v, -700.0)))


K, T, N = 512, 512, 256


def setup_inputs():
    n = np.random.standard_normal
    s = mx_kscale(K)[:, None]
    packed_xT = pack_weight(n((K, T)) * s)
    return {
        "x_words": packed_xT[0],
        "x_scales": packed_xT[1],
        "w1": (n((K, N)) / np.sqrt(K) / s).astype(np.float32),
        "w2": (n((K, N)) / np.sqrt(K) / s).astype(np.float32),
        "w3": (n((K, N)) / np.sqrt(K) / s).astype(np.float32),
        "pos1": striped(np.random.permutation(T)),
        "pos2": striped(np.random.permutation(T)),
        "pos3": striped(np.random.permutation(T)),
        "pos4": striped(np.random.permutation(T)),
    }


def reference(x_words, x_scales, w1, w2, w3, pos1, pos2, pos3, pos4):
    xq = unpack_weight(x_words, x_scales)
    y = mxq(f64(w1), 0, "e4m3").T @ xq
    e = mxq(f64(w2), 0, "e4m3").T @ xq
    h = mxq(f64(w3), 0, "e4m3").T @ xq
    z = (sigmoid(y + e[:, unstriped(pos1)])) * h[:, unstriped(pos1)] + (sigmoid(y + e[:, unstriped(pos2)])) * h[:, unstriped(pos2)] + (sigmoid(y + e[:, unstriped(pos3)])) * h[:, unstriped(pos3)] + (sigmoid(y + e[:, unstriped(pos4)])) * h[:, unstriped(pos4)]
    return z

@@ -1,0 +1,186 @@
+from contextlib import ExitStack
+
+import concourse.mybir as mybir
+from concourse.masks import make_identity
+
+K, T, N, D = 512, 512, 256, 4
+FLOPS = 3 * 2 * K * T * N
+
+F32 = mybir.dt.float32
+BF16 = mybir.dt.bfloat16
+I32 = mybir.dt.int32
+U32 = mybir.dt.uint32
+U16 = mybir.dt.uint16
+U8 = mybir.dt.uint8
+FP8X4 = mybir.dt.float8_e4m3fn_x4
+ADD = mybir.AluOpType.add
+MULT = mybir.AluOpType.mult
+SIGMOID = mybir.ActivationFunctionType.Sigmoid
+
+P = 128
+PACK = 4
+SPARE = 8
+HALF = T // 2
+CHUNKS = T // P
+
+
+def tile_picked_wgatedg_none_l_kernel(
+    tc, x_words, x_scales, w1, w2, w3, pos1, pos2, pos3, pos4, out
+):
+    nc = tc.nc
+    with ExitStack() as ctx:
+        keep = ctx.enter_context(tc.tile_pool(name="keep", bufs=1))
+        psum = ctx.enter_context(tc.psum_pool(name="psum", bufs=1))
+
+        def bank(i):
+            return psum.tile([P, T], F32, name="bank%d" % i)
+
+        lists = [keep.tile([P, T // 16], U16, name="list%d" % d) for d in range(D)]
+        x_codes = [keep.tile([P, HALF], U32, name="x_codes%d" % u, align_bytes=64) for u in range(2)]
+        x_rows = keep.tile([P, T // 4], I32, name="x_rows")
+        x_plane = keep.tile([P, T], U8, name="x_plane", align_bytes=64)
+        warm = keep.tile([P, 2], F32, name="warm")
+        ident = keep.tile([P, P], F32, name="ident")
+        weights = {"y": w1, "e": w2, "h": w3}
+        raw = {}
+        res = {}
+        for b in range(2):
+            for r in ("e", "y", "h"):
+                raw[r, b] = keep.tile([P, PACK, P], F32, name="raw_%s%d" % (r, b))
+                res[r, b] = keep.tile([P, T if r == "y" else T + SPARE], F32, name="res_%s%d" % (r, b))
+
+        def load_w(r, b):
+            nc.sync.dma_start(out=raw[r, b][:], in_=weights[r][:, b * P : (b + 1) * P].rearrange("(p j) m -> p j m", j=PACK))
+
+        x_flat = x_words[0].rearrange("p n t -> p (n t)")
+        load_w("e", 0)
+        for q in range(4):
+            nc.scalar.dma_start(out=x_rows[32 * q : 32 * q + 4, :], in_=x_scales[0, 4 * q : 4 * q + 4, :].bitcast(I32))
+        load_w("y", 0)
+        for u in range(2):
+            nc.sync.dma_start(out=x_codes[u][:].bitcast(I32), in_=x_flat[:, u * HALF * PACK : (u + 1) * HALF * PACK].bitcast(I32))
+        nc.vector.memset(warm[:, 0:1], 0.0)
+        nc.vector.memset(x_plane[:].bitcast(I32), 0)
+        nc.scalar.activation(warm[:, 1:2], warm[:, 0:1], SIGMOID)
+        nc.sync.dma_start(lists[0][:], pos1)
+        load_w("h", 0)
+        nc.sync.dma_start(lists[1][:], pos2)
+        nc.sync.dma_start(lists[2][:], pos3)
+        load_w("e", 1)
+        load_w("y", 1)
+        nc.sync.dma_start(lists[3][:], pos4)
+        load_w("h", 1)
+        for b in range(2):
+            for r in ("e", "h"):
+                nc.gpsimd.memset(res[r, b][:, T:], 0.0)
+        make_identity(nc, ident[:])
+
+        quantised = {}
+
+        def quantise(r, b, on_vector, grouped_tag, codes_tag):
+            grouped = keep.tile([P, P, PACK], BF16, name="grouped_%s%d" % (r, b), tag=grouped_tag, align_bytes=64)
+            src = raw[r, b][:].rearrange("p j m -> p m j")
+            if on_vector:
+                nc.vector.tensor_copy(out=grouped[:], in_=src)
+            else:
+                nc.scalar.copy(out=grouped[:], in_=src)
+            codes = keep.tile([P, P], U32, name="codes_%s%d" % (r, b), tag=codes_tag, align_bytes=64)
+            plane = keep.tile([P, P], U8, name="plane_%s%d" % (r, b), align_bytes=64)
+            nc.vector.quantize_mx(out=codes[:].bitcast(FP8X4), scales=plane[:], in_=grouped[:].rearrange("p m j -> p (m j)"))
+            quantised[r, b] = (codes, plane)
+
+        def product(r, b, u, acc):
+            codes, plane = quantised[r, b]
+            nc.tensor.matmul_mx(out=acc, lhsT=codes[:].bitcast(FP8X4), lhsT_scale=plane[:],
+                                rhs=x_codes[u][:].bitcast(FP8X4), rhs_scale=x_plane[:, u * HALF : (u + 1) * HALF], start=True, stop=True)
+
+        def project(r, b, i):
+            acc = bank(i)
+            for u in range(2):
+                product(r, b, u, acc[:, u * HALF : (u + 1) * HALF])
+            nc.scalar.copy(out=res[r, b][:, :T], in_=acc[:])
+
+        gates = {}
+        msgs = {}
+
+        def gate(b, d, lo, hi, pre=None):
+            if pre is None:
+                pre = keep.tile([P, hi - lo], F32, name="pre%d_%d_%d" % (b, d, lo))[:]
+            if (b, d) not in gates:
+                gates[b, d] = keep.tile([P, T], F32, name="gate%d_%d" % (b, d))
+            nc.vector.tensor_tensor(pre, res["e", b][:].indirect(lists[d][:, lo // 16 : hi // 16]), res["y", b][:, lo:hi], ADD)
+            nc.scalar.activation(gates[b, d][:, lo:hi], pre, SIGMOID)
+
+        def message(b, d, lo, hi):
+            msgs[b, d, lo] = keep.tile([P, hi - lo], F32, name="msg%d_%d_%d" % (b, d, lo))
+            nc.vector.tensor_tensor(msgs[b, d, lo][:], res["h", b][:].indirect(lists[d][:, lo // 16 : hi // 16]), gates[b, d][:, lo:hi], MULT)
+
+        def add_turned(turned, b, d, last):
+            for c in range(CHUNKS):
+                nc.tensor.matmul(turned[c][:, :P], msgs[b, d, 0][:, c * P : (c + 1) * P], ident[:],
+                                 start=(d == 0), stop=(d == last), is_transpose=True)
+
+        def turn_back(turned, b, totals):
+            for c in range(CHUNKS):
+                staged = keep.tile([P, P], F32, name="staged%d_%d" % (b, c))
+                nc.scalar.copy(out=staged[:], in_=turned[c][:, :P])
+                nc.tensor.transpose(totals[c], staged[:], ident[:])
+
+        quantise("e", 0, True, "grouped_e0", "codes_e0")
+        for q in range(4):
+            nc.vector.tensor_copy(out=x_plane[32 * q : 32 * q + 4, :].bitcast(I32), in_=x_rows[32 * q : 32 * q + 4, :])
+        quantise("y", 0, True, "grouped_y0", "codes_y0")
+        first = [bank(i) for i in range(4)]
+        for u in range(2):
+            product("e", 0, u, first[u][:, :HALF])
+            nc.scalar.copy(out=res["e", 0][:, u * HALF : (u + 1) * HALF], in_=first[u][:, :HALF])
+        for u in range(2):
+            product("y", 0, u, first[2 + u][:, :HALF])
+        nc.vector.tensor_copy(out=res["y", 0][:, :HALF], in_=first[2][:, :HALF])
+        nc.scalar.copy(out=res["y", 0][:, HALF:], in_=first[3][:, :HALF])
+        quantise("h", 0, False, "codes_y0", "codes_h0")
+        project("h", 0, 4)
+
+        turned = [bank(c) for c in range(CHUNKS)]
+        gate(0, 0, 0, HALF)
+        gate(0, 0, HALF, T)
+        gate(0, 1, 0, T)
+        quantise("e", 1, False, "grouped_e1", "codes_e1")
+        quantise("y", 1, False, "grouped_y1", "codes_y1")
+        gate(0, 2, 0, T)
+        project("e", 1, 5)
+        project("y", 1, 6)
+        message(0, 0, 0, T)
+        add_turned(turned, 0, 0, D - 1)
+        gate(0, 3, 0, T)
+        quantise("h", 1, False, "grouped_h1", "codes_h1")
+        project("h", 1, 7)
+        message(0, 1, 0, T)
+        add_turned(turned, 0, 1, D - 1)
+        message(0, 2, 0, T)
+        add_turned(turned, 0, 2, D - 1)
+        gate(1, 0, 0, T)
+        message(0, 3, 0, T)
+        add_turned(turned, 0, 3, D - 1)
+        gate(1, 1, 0, T)
+        gate(1, 2, 0, T)
+        total = bank(4)
+        turn_back(turned, 0, [total[:, c * P : (c + 1) * P] for c in range(CHUNKS)])
+        done = keep.tile([P, T], F32, name="done0")
+        nc.scalar.copy(out=done[:], in_=total[:])
+        nc.sync.dma_start(out=out[0:P, :], in_=done[:])
+
+        turned = [bank(c) for c in range(CHUNKS)]
+        for d in range(D - 1):
+            message(1, d, 0, T)
+            add_turned(turned, 1, d, D - 2)
+        for lo in (0, HALF):
+            gate(1, D - 1, lo, lo + HALF, gates[1, D - 2][:, lo : lo + HALF])
+        halves = [bank(5), bank(6)]
+        turn_back(turned, 1, [halves[c // 2][:, (c % 2) * P : (c % 2 + 1) * P] for c in range(CHUNKS)])
+        for lo in (0, HALF):
+            message(1, D - 1, lo, lo + HALF)
+        for u in range(2):
+            done = keep.tile([P, HALF], F32, name="done1_%d" % u)
+            nc.vector.tensor_tensor(done[:], halves[u][:, :HALF], msgs[1, D - 1, u * HALF][:], ADD)
+            nc.sync.dma_start(out=out[P : 2 * P, u * HALF : (u + 1) * HALF], in_=done[:])

@@ -19,7 +19,7 @@ SIGMOID = mybir.ActivationFunctionType.Sigmoid
 
 P = 128
 PACK = 4
-SPARE = 8
+SPARE = 192
 HALF = T // 2
 CHUNKS = T // P
 
@@ -36,33 +36,33 @@ def tile_picked_wgatedg_none_l_kernel(
             return psum.tile([P, T], F32, name="bank%d" % i)
 
         lists = [keep.tile([P, T // 16], U16, name="list%d" % d) for d in range(D)]
-        x_codes = [keep.tile([P, HALF], U32, name="x_codes%d" % u, align_bytes=64) for u in range(2)]
-        x_rows = keep.tile([P, T // 4], I32, name="x_rows")
+        x_codes = keep.tile([P, T], U32, name="x_codes", align_bytes=64)
         x_plane = keep.tile([P, T], U8, name="x_plane", align_bytes=64)
         warm = keep.tile([P, 2], F32, name="warm")
         ident = keep.tile([P, P], F32, name="ident")
         weights = {"y": w1, "e": w2, "h": w3}
         raw = {}
+        for r in ("e", "y", "h"):
+            raw[r, 0] = keep.tile([P, PACK, P], F32, name="raw_%s0" % r, align_bytes=64)[:]
+            raw[r, 1] = keep.tile([P, PACK, P], F32, name="raw_%s1" % r, align_bytes=64)[:]
         res = {}
         for b in range(2):
             for r in ("e", "y", "h"):
-                raw[r, b] = keep.tile([P, PACK, P], F32, name="raw_%s%d" % (r, b))
                 res[r, b] = keep.tile([P, T if r == "y" else T + SPARE], F32, name="res_%s%d" % (r, b))
 
         def load_w(r, b):
-            nc.sync.dma_start(out=raw[r, b][:], in_=weights[r][:, b * P : (b + 1) * P].rearrange("(p j) m -> p j m", j=PACK))
+            nc.sync.dma_start(out=raw[r, b], in_=weights[r][:, b * P : (b + 1) * P].rearrange("(p j) m -> p j m", j=PACK))
 
         x_flat = x_words[0].rearrange("p n t -> p (n t)")
+        nc.vector.memset(x_plane[:].bitcast(I32), 0)
         load_w("e", 0)
         for q in range(4):
-            nc.scalar.dma_start(out=x_rows[32 * q : 32 * q + 4, :], in_=x_scales[0, 4 * q : 4 * q + 4, :].bitcast(I32))
-        load_w("y", 0)
-        for u in range(2):
-            nc.sync.dma_start(out=x_codes[u][:].bitcast(I32), in_=x_flat[:, u * HALF * PACK : (u + 1) * HALF * PACK].bitcast(I32))
-        nc.vector.memset(warm[:, 0:1], 0.0)
-        nc.vector.memset(x_plane[:].bitcast(I32), 0)
-        nc.scalar.activation(warm[:, 1:2], warm[:, 0:1], SIGMOID)
+            nc.scalar.dma_start(out=x_plane[32 * q : 32 * q + 4, :].bitcast(I32), in_=x_scales[0, 4 * q : 4 * q + 4, :].bitcast(I32))
+        nc.sync.dma_start(out=x_codes[:].bitcast(I32), in_=x_flat.bitcast(I32))
         nc.sync.dma_start(lists[0][:], pos1)
+        load_w("y", 0)
+        nc.vector.memset(warm[:, 0:1], 0.0)
+        nc.scalar.activation(warm[:, 1:2], warm[:, 0:1], SIGMOID)
         load_w("h", 0)
         nc.sync.dma_start(lists[1][:], pos2)
         nc.sync.dma_start(lists[2][:], pos3)
@@ -79,7 +79,7 @@ def tile_picked_wgatedg_none_l_kernel(
 
         def quantise(r, b, on_vector, grouped_tag, codes_tag):
             grouped = keep.tile([P, P, PACK], BF16, name="grouped_%s%d" % (r, b), tag=grouped_tag, align_bytes=64)
-            src = raw[r, b][:].rearrange("p j m -> p m j")
+            src = raw[r, b].rearrange("p j m -> p m j")
             if on_vector:
                 nc.vector.tensor_copy(out=grouped[:], in_=src)
             else:
@@ -87,17 +87,16 @@ def tile_picked_wgatedg_none_l_kernel(
             codes = keep.tile([P, P], U32, name="codes_%s%d" % (r, b), tag=codes_tag, align_bytes=64)
             plane = keep.tile([P, P], U8, name="plane_%s%d" % (r, b), align_bytes=64)
             nc.vector.quantize_mx(out=codes[:].bitcast(FP8X4), scales=plane[:], in_=grouped[:].rearrange("p m j -> p (m j)"))
-            quantised[r, b] = (codes, plane)
+            quantised[r, b] = (codes[:], plane[:])
 
-        def product(r, b, u, acc):
+        def product(r, b, lo, hi, acc):
             codes, plane = quantised[r, b]
-            nc.tensor.matmul_mx(out=acc, lhsT=codes[:].bitcast(FP8X4), lhsT_scale=plane[:],
-                                rhs=x_codes[u][:].bitcast(FP8X4), rhs_scale=x_plane[:, u * HALF : (u + 1) * HALF], start=True, stop=True)
+            nc.tensor.matmul_mx(out=acc, lhsT=codes.bitcast(FP8X4), lhsT_scale=plane,
+                                rhs=x_codes[:, lo:hi].bitcast(FP8X4), rhs_scale=x_plane[:, lo:hi], start=True, stop=True)
 
         def project(r, b, i):
             acc = bank(i)
-            for u in range(2):
-                product(r, b, u, acc[:, u * HALF : (u + 1) * HALF])
+            product(r, b, 0, T, acc[:])
             nc.scalar.copy(out=res[r, b][:, :T], in_=acc[:])
 
         gates = {}
@@ -107,7 +106,7 @@ def tile_picked_wgatedg_none_l_kernel(
             if pre is None:
                 pre = keep.tile([P, hi - lo], F32, name="pre%d_%d_%d" % (b, d, lo))[:]
             if (b, d) not in gates:
-                gates[b, d] = keep.tile([P, T], F32, name="gate%d_%d" % (b, d))
+                gates[b, d] = keep.tile([P, T], F32, name="gate%d_%d" % (b, d))[:]
             nc.vector.tensor_tensor(pre, res["e", b][:].indirect(lists[d][:, lo // 16 : hi // 16]), res["y", b][:, lo:hi], ADD)
             nc.scalar.activation(gates[b, d][:, lo:hi], pre, SIGMOID)
 
@@ -115,72 +114,88 @@ def tile_picked_wgatedg_none_l_kernel(
             msgs[b, d, lo] = keep.tile([P, hi - lo], F32, name="msg%d_%d_%d" % (b, d, lo))
             nc.vector.tensor_tensor(msgs[b, d, lo][:], res["h", b][:].indirect(lists[d][:, lo // 16 : hi // 16]), gates[b, d][:, lo:hi], MULT)
 
-        def add_turned(turned, b, d, last):
+        def add_turned(turned, b, d, first, last):
             for c in range(CHUNKS):
                 nc.tensor.matmul(turned[c][:, :P], msgs[b, d, 0][:, c * P : (c + 1) * P], ident[:],
-                                 start=(d == 0), stop=(d == last), is_transpose=True)
+                                 start=(d == first), stop=(d == last), is_transpose=True)
 
-        def turn_back(turned, b, totals):
-            for c in range(CHUNKS):
+        def turn_back(turned, b, totals, chunks):
+            for c in chunks:
                 staged = keep.tile([P, P], F32, name="staged%d_%d" % (b, c))
                 nc.scalar.copy(out=staged[:], in_=turned[c][:, :P])
                 nc.tensor.transpose(totals[c], staged[:], ident[:])
 
         quantise("e", 0, True, "grouped_e0", "codes_e0")
-        for q in range(4):
-            nc.vector.tensor_copy(out=x_plane[32 * q : 32 * q + 4, :].bitcast(I32), in_=x_rows[32 * q : 32 * q + 4, :])
-        quantise("y", 0, True, "grouped_y0", "codes_y0")
         first = [bank(i) for i in range(4)]
         for u in range(2):
-            product("e", 0, u, first[u][:, :HALF])
-            nc.scalar.copy(out=res["e", 0][:, u * HALF : (u + 1) * HALF], in_=first[u][:, :HALF])
+            product("e", 0, u * HALF, (u + 1) * HALF, first[u][:, :HALF])
+        nc.scalar.copy(out=res["e", 0][:, :HALF], in_=first[0][:, :HALF])
+        quantise("y", 0, True, "grouped_y0", "codes_y0")
+        nc.vector.tensor_copy(out=res["e", 0][:, HALF:T], in_=first[1][:, :HALF])
+        fetched = keep.tile([P, T], F32, name="fetched", tag="raw_y0", align_bytes=64)
+        nc.vector.tensor_copy(fetched[:], res["e", 0][:].indirect(lists[0][:]))
         for u in range(2):
-            product("y", 0, u, first[2 + u][:, :HALF])
-        nc.vector.tensor_copy(out=res["y", 0][:, :HALF], in_=first[2][:, :HALF])
-        nc.scalar.copy(out=res["y", 0][:, HALF:], in_=first[3][:, :HALF])
+            product("y", 0, u * HALF, (u + 1) * HALF, first[2 + u][:, :HALF])
+            nc.scalar.copy(out=res["y", 0][:, u * HALF : (u + 1) * HALF], in_=first[2 + u][:, :HALF])
         quantise("h", 0, False, "codes_y0", "codes_h0")
         project("h", 0, 4)
+        gate(0, 1, 0, HALF)
+        gate(0, 1, HALF, T)
+
+        pre_turned = bank(5)
+        for c in range(CHUNKS):
+            cols = slice(c * P, (c + 1) * P)
+            nc.tensor.matmul(pre_turned[:, cols], fetched[:, cols], ident[:], start=True, stop=False, is_transpose=True)
+            nc.tensor.matmul(pre_turned[:, cols], res["y", 0][:, cols], ident[:], start=False, stop=True, is_transpose=True)
+        gate_turned = keep.tile([P, T], F32, name="gate_turned", align_bytes=64)
+        nc.scalar.activation(gate_turned[:], pre_turned[:], SIGMOID)
+        gate_back = bank(6)
+        for c in range(CHUNKS):
+            cols = slice(c * P, (c + 1) * P)
+            nc.tensor.transpose(gate_back[:, cols], gate_turned[:, cols], ident[:])
+        gates[0, 0] = keep.tile([P, T], F32, name="gate0_0")[:]
+        nc.scalar.copy(out=gates[0, 0][:], in_=gate_back[:])
 
         turned = [bank(c) for c in range(CHUNKS)]
-        gate(0, 0, 0, HALF)
-        gate(0, 0, HALF, T)
-        gate(0, 1, 0, T)
-        quantise("e", 1, False, "grouped_e1", "codes_e1")
-        quantise("y", 1, False, "grouped_y1", "codes_y1")
-        gate(0, 2, 0, T)
-        project("e", 1, 5)
-        project("y", 1, 6)
-        message(0, 0, 0, T)
-        add_turned(turned, 0, 0, D - 1)
-        gate(0, 3, 0, T)
-        quantise("h", 1, False, "grouped_h1", "codes_h1")
-        project("h", 1, 7)
+        gates[0, 2] = keep.tile([P, T], F32, name="gate0_2", tag="raw_e1", align_bytes=64)[:]
+        gates[0, 3] = keep.tile([P, T], F32, name="gate0_3", tag="raw_y1", align_bytes=64)[:]
         message(0, 1, 0, T)
-        add_turned(turned, 0, 1, D - 1)
+        add_turned(turned, 0, 1, 1, D - 1)
+        quantise("e", 1, False, "grouped_e1", "codes_e1")
+        gate(0, 2, 0, T, keep.tile([P, T], F32, name="pre0_2", tag="raw_h0", align_bytes=64)[:])
+        quantise("y", 1, False, "grouped_y1", "codes_y1")
+        gate(0, 3, 0, T, keep.tile([P, T], F32, name="pre0_3", align_bytes=64)[:])
+        project("e", 1, 7)
+        project("y", 1, 4)
         message(0, 2, 0, T)
-        add_turned(turned, 0, 2, D - 1)
-        gate(1, 0, 0, T)
+        add_turned(turned, 0, 2, 1, D - 1)
+        message(0, 0, 0, T)
+        add_turned(turned, 0, 0, 1, D - 1)
+        quantise("h", 1, False, "pre0_3", "codes_h1")
+        project("h", 1, 5)
         message(0, 3, 0, T)
-        add_turned(turned, 0, 3, D - 1)
-        gate(1, 1, 0, T)
-        gate(1, 2, 0, T)
-        total = bank(4)
-        turn_back(turned, 0, [total[:, c * P : (c + 1) * P] for c in range(CHUNKS)])
+        add_turned(turned, 0, 3, 1, D - 1)
+        total = bank(6)
+        turn_back(turned, 0, [total[:, c * P : (c + 1) * P] for c in range(CHUNKS)], range(CHUNKS))
         done = keep.tile([P, T], F32, name="done0")
         nc.scalar.copy(out=done[:], in_=total[:])
         nc.sync.dma_start(out=out[0:P, :], in_=done[:])
+        gate(1, 0, 0, T)
+        gates[1, 1] = keep.tile([P, T], F32, name="gate1_1", tag="codes_h1", align_bytes=64)[:]
+        gate(1, 1, 0, T)
+        gate(1, 2, 0, T)
 
         turned = [bank(c) for c in range(CHUNKS)]
         for d in range(D - 1):
             message(1, d, 0, T)
-            add_turned(turned, 1, d, D - 2)
-        for lo in (0, HALF):
-            gate(1, D - 1, lo, lo + HALF, gates[1, D - 2][:, lo : lo + HALF])
-        halves = [bank(5), bank(6)]
-        turn_back(turned, 1, [halves[c // 2][:, (c % 2) * P : (c % 2 + 1) * P] for c in range(CHUNKS)])
+            add_turned(turned, 1, d, 0, D - 2)
+        halves = [bank(4), bank(7)]
+        for u in range(2):
+            gate(1, D - 1, u * HALF, (u + 1) * HALF, gates[1, D - 3][:, u * HALF : (u + 1) * HALF])
+            turn_back(turned, 1, [halves[c // 2][:, (c % 2) * P : (c % 2 + 1) * P] for c in range(CHUNKS)], (2 * u, 2 * u + 1))
         for lo in (0, HALF):
             message(1, D - 1, lo, lo + HALF)
         for u in range(2):
             done = keep.tile([P, HALF], F32, name="done1_%d" % u)
             nc.vector.tensor_tensor(done[:], halves[u][:, :HALF], msgs[1, D - 1, u * HALF][:], ADD)
-            nc.sync.dma_start(out=out[P : 2 * P, u * HALF : (u + 1) * HALF], in_=done[:])
+            (nc.sync if u == 0 else nc.scalar).dma_start(out=out[P : 2 * P, u * HALF : (u + 1) * HALF], in_=done[:])

@@ -19,7 +19,8 @@ SIGMOID = mybir.ActivationFunctionType.Sigmoid
 
 P = 128
 PACK = 4
-SPARE = 192
+SPARE = 8
+WIDE_SPARE = 192
 HALF = T // 2
 CHUNKS = T // P
 
@@ -48,20 +49,20 @@ def tile_picked_wgatedg_none_l_kernel(
         res = {}
         for b in range(2):
             for r in ("e", "y", "h"):
-                res[r, b] = keep.tile([P, T if r == "y" else T + SPARE], F32, name="res_%s%d" % (r, b))
+                res[r, b] = keep.tile([P, T if r == "y" else T + (WIDE_SPARE if (r, b) == ("e", 0) else SPARE)], F32, name="res_%s%d" % (r, b))
 
         def load_w(r, b):
             nc.sync.dma_start(out=raw[r, b], in_=weights[r][:, b * P : (b + 1) * P].rearrange("(p j) m -> p j m", j=PACK))
 
         x_flat = x_words[0].rearrange("p n t -> p (n t)")
-        nc.vector.memset(x_plane[:].bitcast(I32), 0)
+        nc.gpsimd.memset(x_plane[:].bitcast(I32), 0)
         load_w("e", 0)
         for q in range(4):
             nc.scalar.dma_start(out=x_plane[32 * q : 32 * q + 4, :].bitcast(I32), in_=x_scales[0, 4 * q : 4 * q + 4, :].bitcast(I32))
         nc.sync.dma_start(out=x_codes[:].bitcast(I32), in_=x_flat.bitcast(I32))
         nc.sync.dma_start(lists[0][:], pos1)
         load_w("y", 0)
-        nc.vector.memset(warm[:, 0:1], 0.0)
+        nc.gpsimd.memset(warm[:, 0:1], 0.0)
         nc.scalar.activation(warm[:, 1:2], warm[:, 0:1], SIGMOID)
         load_w("h", 0)
         nc.sync.dma_start(lists[1][:], pos2)
@@ -102,17 +103,40 @@ def tile_picked_wgatedg_none_l_kernel(
         gates = {}
         msgs = {}
 
-        def gate(b, d, lo, hi, pre=None):
+        def gate(b, d, lo, hi, pre=None, dst=None):
             if pre is None:
                 pre = keep.tile([P, hi - lo], F32, name="pre%d_%d_%d" % (b, d, lo))[:]
             if (b, d) not in gates:
                 gates[b, d] = keep.tile([P, T], F32, name="gate%d_%d" % (b, d))[:]
             nc.vector.tensor_tensor(pre, res["e", b][:].indirect(lists[d][:, lo // 16 : hi // 16]), res["y", b][:, lo:hi], ADD)
-            nc.scalar.activation(gates[b, d][:, lo:hi], pre, SIGMOID)
+            nc.scalar.activation(gates[b, d][:, lo:hi] if dst is None else dst, pre, SIGMOID)
 
-        def message(b, d, lo, hi):
-            msgs[b, d, lo] = keep.tile([P, hi - lo], F32, name="msg%d_%d_%d" % (b, d, lo))
-            nc.vector.tensor_tensor(msgs[b, d, lo][:], res["h", b][:].indirect(lists[d][:, lo // 16 : hi // 16]), gates[b, d][:, lo:hi], MULT)
+        fetched = {}
+
+        def fetch(b, d, tag):
+            fetched[b, d] = keep.tile([P, T], F32, name="fetched%d_%d" % (b, d), tag=tag, align_bytes=64)
+            nc.vector.tensor_copy(fetched[b, d][:], res["e", b][:].indirect(lists[d][:]))
+
+        def turned_gate(b, d, i, j):
+            pre_turned = bank(i)
+            for c in range(CHUNKS):
+                cols = slice(c * P, (c + 1) * P)
+                nc.tensor.matmul(pre_turned[:, cols], res["y", b][:, cols], ident[:], start=True, stop=False, is_transpose=True)
+                nc.tensor.matmul(pre_turned[:, cols], fetched[b, d][:, cols], ident[:], start=False, stop=True, is_transpose=True)
+            gate_turned = keep.tile([P, T], F32, name="gate_turned%d_%d" % (b, d))
+            nc.scalar.activation(gate_turned[:], pre_turned[:], SIGMOID)
+            gate_back = bank(j)
+            for c in range(CHUNKS):
+                cols = slice(c * P, (c + 1) * P)
+                nc.tensor.transpose(gate_back[:, cols], gate_turned[:, cols], ident[:])
+            if (b, d) not in gates:
+                gates[b, d] = keep.tile([P, T], F32, name="gate%d_%d" % (b, d))[:]
+            nc.scalar.copy(out=gates[b, d], in_=gate_back[:])
+
+        def message(b, d, lo, hi, src=None):
+            if (b, d, lo) not in msgs:
+                msgs[b, d, lo] = keep.tile([P, hi - lo], F32, name="msg%d_%d_%d" % (b, d, lo))[:]
+            nc.vector.tensor_tensor(msgs[b, d, lo][:], res["h", b][:].indirect(lists[d][:, lo // 16 : hi // 16]), gates[b, d][:, lo:hi] if src is None else src, MULT)
 
         def add_turned(turned, b, d, first, last):
             for c in range(CHUNKS):
@@ -127,13 +151,15 @@ def tile_picked_wgatedg_none_l_kernel(
 
         quantise("e", 0, True, "grouped_e0", "codes_e0")
         first = [bank(i) for i in range(4)]
-        for u in range(2):
-            product("e", 0, u * HALF, (u + 1) * HALF, first[u][:, :HALF])
+        extra = bank(7)
+        product("e", 0, 0, HALF, first[0][:, :HALF])
+        product("e", 0, HALF, HALF + P, first[1][:, :P])
+        product("e", 0, HALF + P, T, extra[:, :P])
         nc.scalar.copy(out=res["e", 0][:, :HALF], in_=first[0][:, :HALF])
+        nc.vector.tensor_copy(out=res["e", 0][:, HALF : HALF + P], in_=first[1][:, :P])
+        nc.vector.tensor_copy(out=res["e", 0][:, HALF + P : T], in_=extra[:, :P])
         quantise("y", 0, True, "grouped_y0", "codes_y0")
-        nc.vector.tensor_copy(out=res["e", 0][:, HALF:T], in_=first[1][:, :HALF])
-        fetched = keep.tile([P, T], F32, name="fetched", tag="raw_y0", align_bytes=64)
-        nc.vector.tensor_copy(fetched[:], res["e", 0][:].indirect(lists[0][:]))
+        fetch(0, 0, "raw_y0")
         for u in range(2):
             product("y", 0, u * HALF, (u + 1) * HALF, first[2 + u][:, :HALF])
             nc.scalar.copy(out=res["y", 0][:, u * HALF : (u + 1) * HALF], in_=first[2 + u][:, :HALF])
@@ -142,19 +168,7 @@ def tile_picked_wgatedg_none_l_kernel(
         gate(0, 1, 0, HALF)
         gate(0, 1, HALF, T)
 
-        pre_turned = bank(5)
-        for c in range(CHUNKS):
-            cols = slice(c * P, (c + 1) * P)
-            nc.tensor.matmul(pre_turned[:, cols], fetched[:, cols], ident[:], start=True, stop=False, is_transpose=True)
-            nc.tensor.matmul(pre_turned[:, cols], res["y", 0][:, cols], ident[:], start=False, stop=True, is_transpose=True)
-        gate_turned = keep.tile([P, T], F32, name="gate_turned", align_bytes=64)
-        nc.scalar.activation(gate_turned[:], pre_turned[:], SIGMOID)
-        gate_back = bank(6)
-        for c in range(CHUNKS):
-            cols = slice(c * P, (c + 1) * P)
-            nc.tensor.transpose(gate_back[:, cols], gate_turned[:, cols], ident[:])
-        gates[0, 0] = keep.tile([P, T], F32, name="gate0_0")[:]
-        nc.scalar.copy(out=gates[0, 0][:], in_=gate_back[:])
+        turned_gate(0, 0, 5, 6)
 
         turned = [bank(c) for c in range(CHUNKS)]
         gates[0, 2] = keep.tile([P, T], F32, name="gate0_2", tag="raw_e1", align_bytes=64)[:]
@@ -183,19 +197,31 @@ def tile_picked_wgatedg_none_l_kernel(
         gate(1, 0, 0, T)
         gates[1, 1] = keep.tile([P, T], F32, name="gate1_1", tag="codes_h1", align_bytes=64)[:]
         gate(1, 1, 0, T)
+        shared = keep.tile([P, T + HALF], F32, name="shared")
+        gates[1, 2] = shared[:, :T]
         gate(1, 2, 0, T)
+        gate(1, D - 1, 0, HALF)
 
         turned = [bank(c) for c in range(CHUNKS)]
-        for d in range(D - 1):
+        for d in range(D - 2):
             message(1, d, 0, T)
             add_turned(turned, 1, d, 0, D - 2)
-        halves = [bank(4), bank(7)]
+        front, back = bank(4), bank(7)
+        targets = [front[:, c * P : (c + 1) * P] for c in range(CHUNKS - 1)] + [back[:, :P]]
+        pieces = [(0, 2, front[:, : 2 * P]), (2, 3, targets[2]), (3, 4, targets[3])]
         for u in range(2):
-            gate(1, D - 1, u * HALF, (u + 1) * HALF, gates[1, D - 3][:, u * HALF : (u + 1) * HALF])
-            turn_back(turned, 1, [halves[c // 2][:, (c % 2) * P : (c % 2 + 1) * P] for c in range(CHUNKS)], (2 * u, 2 * u + 1))
-        for lo in (0, HALF):
-            message(1, D - 1, lo, lo + HALF)
-        for u in range(2):
-            done = keep.tile([P, HALF], F32, name="done1_%d" % u)
-            nc.vector.tensor_tensor(done[:], halves[u][:, :HALF], msgs[1, D - 1, u * HALF][:], ADD)
-            (nc.sync if u == 0 else nc.scalar).dma_start(out=out[P : 2 * P, u * HALF : (u + 1) * HALF], in_=done[:])
+            message(1, D - 2, u * HALF, (u + 1) * HALF)
+            for c in (2 * u, 2 * u + 1):
+                nc.tensor.matmul(turned[c][:, :P], msgs[1, D - 2, u * HALF][:, (c % 2) * P : (c % 2 + 1) * P], ident[:],
+                                 start=False, stop=True, is_transpose=True)
+        turn_back(turned, 1, targets, (0, 1))
+        gate(1, D - 1, HALF, T, gates[1, D - 2][:, :HALF], msgs[1, D - 2, 0])
+        turn_back(turned, 1, targets, (2, 3))
+        msgs[1, D - 1, 0] = shared[:, HALF:T]
+        msgs[1, D - 1, HALF] = shared[:, T:]
+        message(1, D - 1, 0, HALF)
+        message(1, D - 1, HALF, T, msgs[1, D - 2, 0])
+        for lo, hi, acc in pieces:
+            done = keep.tile([P, (hi - lo) * P], F32, name="done1_%d" % lo)
+            nc.vector.tensor_tensor(done[:], acc, shared[:, HALF + lo * P : HALF + hi * P], ADD)
+            (nc.scalar if lo == 2 else nc.sync).dma_start(out=out[P : 2 * P, lo * P : hi * P], in_=done[:])

from contextlib import ExitStack

import concourse.mybir as mybir
from concourse.masks import make_identity

K, T, N, D = 512, 512, 256, 4
FLOPS = 3 * 2 * K * T * N

F32 = mybir.dt.float32
BF16 = mybir.dt.bfloat16
I32 = mybir.dt.int32
U32 = mybir.dt.uint32
U16 = mybir.dt.uint16
U8 = mybir.dt.uint8
FP8X4 = mybir.dt.float8_e4m3fn_x4
ADD = mybir.AluOpType.add
MULT = mybir.AluOpType.mult
SIGMOID = mybir.ActivationFunctionType.Sigmoid

P = 128
PACK = 4
SPARE = 8
WIDE_SPARE = 192
HALF = T // 2
CHUNKS = T // P


def tile_picked_wgatedg_none_l_kernel(
    tc, x_words, x_scales, w1, w2, w3, pos1, pos2, pos3, pos4, out
):
    nc = tc.nc
    with ExitStack() as ctx:
        keep = ctx.enter_context(tc.tile_pool(name="keep", bufs=1))
        psum = ctx.enter_context(tc.psum_pool(name="psum", bufs=1))

        def bank(i):
            return psum.tile([P, T], F32, name="bank%d" % i)

        lists = [keep.tile([P, T // 16], U16, name="list%d" % d) for d in range(D)]
        x_codes = keep.tile([P, T], U32, name="x_codes", align_bytes=64)
        x_plane = keep.tile([P, T], U8, name="x_plane", align_bytes=64)
        warm = keep.tile([P, 2], F32, name="warm")
        ident = keep.tile([P, P], F32, name="ident")
        weights = {"y": w1, "e": w2, "h": w3}
        raw = {}
        for r in ("e", "y", "h"):
            raw[r, 0] = keep.tile([P, PACK, P], F32, name="raw_%s0" % r, align_bytes=64)[:]
            raw[r, 1] = keep.tile([P, PACK, P], F32, name="raw_%s1" % r, align_bytes=64)[:]
        res = {}
        for b in range(2):
            for r in ("e", "y", "h"):
                res[r, b] = keep.tile([P, T if r == "y" else T + (WIDE_SPARE if (r, b) == ("e", 0) else SPARE)], F32, name="res_%s%d" % (r, b))

        def load_w(r, b):
            nc.sync.dma_start(out=raw[r, b], in_=weights[r][:, b * P : (b + 1) * P].rearrange("(p j) m -> p j m", j=PACK))

        x_flat = x_words[0].rearrange("p n t -> p (n t)")
        nc.gpsimd.memset(x_plane[:].bitcast(I32), 0)
        load_w("e", 0)
        for q in range(4):
            nc.scalar.dma_start(out=x_plane[32 * q : 32 * q + 4, :].bitcast(I32), in_=x_scales[0, 4 * q : 4 * q + 4, :].bitcast(I32))
        nc.sync.dma_start(out=x_codes[:].bitcast(I32), in_=x_flat.bitcast(I32))
        nc.sync.dma_start(lists[0][:], pos1)
        load_w("y", 0)
        nc.gpsimd.memset(warm[:, 0:1], 0.0)
        nc.scalar.activation(warm[:, 1:2], warm[:, 0:1], SIGMOID)
        load_w("h", 0)
        nc.sync.dma_start(lists[1][:], pos2)
        nc.sync.dma_start(lists[2][:], pos3)
        load_w("e", 1)
        load_w("y", 1)
        nc.sync.dma_start(lists[3][:], pos4)
        load_w("h", 1)
        for b in range(2):
            for r in ("e", "h"):
                nc.gpsimd.memset(res[r, b][:, T:], 0.0)
        make_identity(nc, ident[:])

        quantised = {}

        def quantise(r, b, on_vector, grouped_tag, codes_tag):
            grouped = keep.tile([P, P, PACK], BF16, name="grouped_%s%d" % (r, b), tag=grouped_tag, align_bytes=64)
            src = raw[r, b].rearrange("p j m -> p m j")
            if on_vector:
                nc.vector.tensor_copy(out=grouped[:], in_=src)
            else:
                nc.scalar.copy(out=grouped[:], in_=src)
            codes = keep.tile([P, P], U32, name="codes_%s%d" % (r, b), tag=codes_tag, align_bytes=64)
            plane = keep.tile([P, P], U8, name="plane_%s%d" % (r, b), align_bytes=64)
            nc.vector.quantize_mx(out=codes[:].bitcast(FP8X4), scales=plane[:], in_=grouped[:].rearrange("p m j -> p (m j)"))
            quantised[r, b] = (codes[:], plane[:])

        def product(r, b, lo, hi, acc):
            codes, plane = quantised[r, b]
            nc.tensor.matmul_mx(out=acc, lhsT=codes.bitcast(FP8X4), lhsT_scale=plane,
                                rhs=x_codes[:, lo:hi].bitcast(FP8X4), rhs_scale=x_plane[:, lo:hi], start=True, stop=True)

        def project(r, b, i):
            acc = bank(i)
            product(r, b, 0, T, acc[:])
            nc.scalar.copy(out=res[r, b][:, :T], in_=acc[:])

        gates = {}
        msgs = {}

        def gate(b, d, lo, hi, pre=None, dst=None):
            if pre is None:
                pre = keep.tile([P, hi - lo], F32, name="pre%d_%d_%d" % (b, d, lo))[:]
            if (b, d) not in gates:
                gates[b, d] = keep.tile([P, T], F32, name="gate%d_%d" % (b, d))[:]
            nc.vector.tensor_tensor(pre, res["e", b][:].indirect(lists[d][:, lo // 16 : hi // 16]), res["y", b][:, lo:hi], ADD)
            nc.scalar.activation(gates[b, d][:, lo:hi] if dst is None else dst, pre, SIGMOID)

        fetched = {}

        def fetch(b, d, tag):
            fetched[b, d] = keep.tile([P, T], F32, name="fetched%d_%d" % (b, d), tag=tag, align_bytes=64)
            nc.vector.tensor_copy(fetched[b, d][:], res["e", b][:].indirect(lists[d][:]))

        def turned_gate(b, d, i, j):
            pre_turned = bank(i)
            for c in range(CHUNKS):
                cols = slice(c * P, (c + 1) * P)
                nc.tensor.matmul(pre_turned[:, cols], res["y", b][:, cols], ident[:], start=True, stop=False, is_transpose=True)
                nc.tensor.matmul(pre_turned[:, cols], fetched[b, d][:, cols], ident[:], start=False, stop=True, is_transpose=True)
            gate_turned = keep.tile([P, T], F32, name="gate_turned%d_%d" % (b, d))
            nc.scalar.activation(gate_turned[:], pre_turned[:], SIGMOID)
            gate_back = bank(j)
            for c in range(CHUNKS):
                cols = slice(c * P, (c + 1) * P)
                nc.tensor.transpose(gate_back[:, cols], gate_turned[:, cols], ident[:])
            if (b, d) not in gates:
                gates[b, d] = keep.tile([P, T], F32, name="gate%d_%d" % (b, d))[:]
            nc.scalar.copy(out=gates[b, d], in_=gate_back[:])

        def message(b, d, lo, hi, src=None):
            if (b, d, lo) not in msgs:
                msgs[b, d, lo] = keep.tile([P, hi - lo], F32, name="msg%d_%d_%d" % (b, d, lo))[:]
            nc.vector.tensor_tensor(msgs[b, d, lo][:], res["h", b][:].indirect(lists[d][:, lo // 16 : hi // 16]), gates[b, d][:, lo:hi] if src is None else src, MULT)

        def add_turned(turned, b, d, first, last):
            for c in range(CHUNKS):
                nc.tensor.matmul(turned[c][:, :P], msgs[b, d, 0][:, c * P : (c + 1) * P], ident[:],
                                 start=(d == first), stop=(d == last), is_transpose=True)

        def turn_back(turned, b, totals, chunks):
            for c in chunks:
                staged = keep.tile([P, P], F32, name="staged%d_%d" % (b, c))
                nc.scalar.copy(out=staged[:], in_=turned[c][:, :P])
                nc.tensor.transpose(totals[c], staged[:], ident[:])

        quantise("e", 0, True, "grouped_e0", "codes_e0")
        first = [bank(i) for i in range(4)]
        extra = bank(7)
        product("e", 0, 0, HALF, first[0][:, :HALF])
        product("e", 0, HALF, HALF + P, first[1][:, :P])
        product("e", 0, HALF + P, T, extra[:, :P])
        nc.scalar.copy(out=res["e", 0][:, :HALF], in_=first[0][:, :HALF])
        nc.vector.tensor_copy(out=res["e", 0][:, HALF : HALF + P], in_=first[1][:, :P])
        nc.vector.tensor_copy(out=res["e", 0][:, HALF + P : T], in_=extra[:, :P])
        quantise("y", 0, True, "grouped_y0", "codes_y0")
        fetch(0, 0, "raw_y0")
        for u in range(2):
            product("y", 0, u * HALF, (u + 1) * HALF, first[2 + u][:, :HALF])
            nc.scalar.copy(out=res["y", 0][:, u * HALF : (u + 1) * HALF], in_=first[2 + u][:, :HALF])
        quantise("h", 0, False, "codes_y0", "codes_h0")
        project("h", 0, 4)
        gate(0, 1, 0, HALF)
        gate(0, 1, HALF, T)

        turned_gate(0, 0, 5, 6)

        turned = [bank(c) for c in range(CHUNKS)]
        gates[0, 2] = keep.tile([P, T], F32, name="gate0_2", tag="raw_e1", align_bytes=64)[:]
        gates[0, 3] = keep.tile([P, T], F32, name="gate0_3", tag="raw_y1", align_bytes=64)[:]
        message(0, 1, 0, T)
        add_turned(turned, 0, 1, 1, D - 1)
        quantise("e", 1, False, "grouped_e1", "codes_e1")
        gate(0, 2, 0, T, keep.tile([P, T], F32, name="pre0_2", tag="raw_h0", align_bytes=64)[:])
        quantise("y", 1, False, "grouped_y1", "codes_y1")
        gate(0, 3, 0, T, keep.tile([P, T], F32, name="pre0_3", align_bytes=64)[:])
        project("e", 1, 7)
        project("y", 1, 4)
        message(0, 2, 0, T)
        add_turned(turned, 0, 2, 1, D - 1)
        message(0, 0, 0, T)
        add_turned(turned, 0, 0, 1, D - 1)
        quantise("h", 1, False, "pre0_3", "codes_h1")
        project("h", 1, 5)
        message(0, 3, 0, T)
        add_turned(turned, 0, 3, 1, D - 1)
        total = bank(6)
        turn_back(turned, 0, [total[:, c * P : (c + 1) * P] for c in range(CHUNKS)], range(CHUNKS))
        done = keep.tile([P, T], F32, name="done0")
        nc.scalar.copy(out=done[:], in_=total[:])
        nc.sync.dma_start(out=out[0:P, :], in_=done[:])
        gate(1, 0, 0, T)
        gates[1, 1] = keep.tile([P, T], F32, name="gate1_1", tag="codes_h1", align_bytes=64)[:]
        gate(1, 1, 0, T)
        shared = keep.tile([P, T + HALF], F32, name="shared")
        gates[1, 2] = shared[:, :T]
        gate(1, 2, 0, T)
        gate(1, D - 1, 0, HALF)

        turned = [bank(c) for c in range(CHUNKS)]
        for d in range(D - 2):
            message(1, d, 0, T)
            add_turned(turned, 1, d, 0, D - 2)
        front, back = bank(4), bank(7)
        targets = [front[:, c * P : (c + 1) * P] for c in range(CHUNKS - 1)] + [back[:, :P]]
        pieces = [(0, 2, front[:, : 2 * P]), (2, 3, targets[2]), (3, 4, targets[3])]
        for u in range(2):
            message(1, D - 2, u * HALF, (u + 1) * HALF)
            for c in (2 * u, 2 * u + 1):
                nc.tensor.matmul(turned[c][:, :P], msgs[1, D - 2, u * HALF][:, (c % 2) * P : (c % 2 + 1) * P], ident[:],
                                 start=False, stop=True, is_transpose=True)
        turn_back(turned, 1, targets, (0, 1))
        gate(1, D - 1, HALF, T, gates[1, D - 2][:, :HALF], msgs[1, D - 2, 0])
        turn_back(turned, 1, targets, (2, 3))
        msgs[1, D - 1, 0] = shared[:, HALF:T]
        msgs[1, D - 1, HALF] = shared[:, T:]
        message(1, D - 1, 0, HALF)
        message(1, D - 1, HALF, T, msgs[1, D - 2, 0])
        for lo, hi, acc in pieces:
            done = keep.tile([P, (hi - lo) * P], F32, name="done1_%d" % lo)
            nc.vector.tensor_tensor(done[:], acc, shared[:, HALF + lo * P : HALF + hi * P], ADD)
            (nc.scalar if lo == 2 else nc.sync).dma_start(out=out[P : 2 * P, lo * P : hi * P], in_=done[:])
